import numpy as np, ml_dtypes
CORES = [23,39,55,63,87,103,111,127,18,34,50,58,82,98,106,122]
N = 16
QP = 64
def setup_inputs(rng):
    return {"q": rng.standard_normal((N, 128, QP), dtype=np.float32).astype(ml_dtypes.bfloat16), "k": rng.standard_normal((N, 128, 128), dtype=np.float32).astype(ml_dtypes.bfloat16), "v": rng.standard_normal((N, 128, 128), dtype=np.float32).astype(ml_dtypes.bfloat16)}
def setup_inputs_big(rng):
    d = setup_inputs(rng)
    for k in ("q", "k", "v"): d[k] = (d[k].astype(np.float32) * 1024.0).astype(d[k].dtype)
    return d
def setup_inputs_small(rng):
    d = setup_inputs(rng)
    for k in ("q", "k", "v"): d[k] = (d[k].astype(np.float32) * (1 / 1024.0)).astype(d[k].dtype)
    return d
def setup_inputs_apart(rng):
    d = setup_inputs(rng)
    f = (10.0 ** rng.permutation(np.linspace(-1.5, 1.5, N))).astype(np.float32).reshape(N, 1, 1)
    for k in ("q", "k", "v"): d[k] = (d[k].astype(np.float32) * f).astype(d[k].dtype)
    return d
def reference(q, k, v):
    Q, K, V = q.astype(np.float64), k.astype(np.float64), v.astype(np.float64)
    y = np.zeros((N, 128, QP))
    for r in range(N):
        S = [K[j].T @ Q[r] for j in range(N)]
        m = np.max([s.max(axis=0) for s in S], axis=0)
        y[r] = sum(V[j].T @ np.maximum(S[j] - 0.5 * m, 0.0) for j in range(N))
    return {"y": y.astype(ml_dtypes.bfloat16)}

@@ -1,0 +1,192 @@
+from concourse.bass import DstId, RemoteDMATransfer
+from concourse.mybir import AluOpType
+
+NB = 16
+W = 256
+QP = 64
+BATCHES = [[0], [1, 2], [3, 4], [5, 6], [7]]
+NT = 3
+
+SCRATCH = {
+    "kv": ("sbuf", [128, NB * W], "bfloat16"),
+    "qs": ("sbuf", [128, QP], "bfloat16"),
+    "ida": ("sbuf", [128, 129], "bfloat16"),
+    "idd": ("dram", [129, 128], "bfloat16"),
+    "ident": ("sbuf", [128, 128], "bfloat16"),
+    "ones": ("sbuf", [128, 8], "bfloat16"),
+    "half": ("sbuf", [128, 128], "bfloat16"),
+    "negh": ("sbuf", [128, QP], "float32"),
+    "acc": ("sbuf", [128, QP], "float32"),
+    "mcol": ("sbuf", [128, 8], "bfloat16"),
+    "mrow": ("sbuf", [128, QP], "bfloat16"),
+    "nhrow": ("sbuf", [128, QP], "float32"),
+    "vsrow": ("sbuf", [128, 128], "float32"),
+    "hb": ("sbuf", [128, QP], "bfloat16"),
+    "pp": ("sbuf", [128, NB * QP], "bfloat16"),
+    "ysb": ("sbuf", [128, QP], "bfloat16"),
+    "pS0": ("psum", [128, 512], "float32"),
+    "pS1": ("psum", [128, 512], "float32"),
+    "pT0": ("psum", [128, 512], "float32"),
+    "pT1": ("psum", [128, 512], "float32"),
+    "pT2": ("psum", [128, 512], "float32"),
+    "pV": ("psum", [128, 512], "float32"),
+    "pY": ("psum", [128, 512], "float32"),
+}
+SEMAPHORES = (["a%d" % i for i in range(8)] + ["f%d" % i for i in range(len(BATCHES))] +
+              ["ld", "ldq", "vi", "di", "di2", "vc", "st", "ss", "sv", "vacc", "vm", "sm", "vrow", "vx", "sh", "vh",
+               "sp", "sy", "vy", "sto", "sent"])
+
+
+def _bits(m):
+    return bin(m).count("1")
+
+
+def rank_program(g, core, T, topo):
+    if T.rank_of(core) is None:
+        return
+    sem = T.sem
+    te, ve, sy, sc = g.tensor, g.vector, g.sync, g.scalar
+
+    chips = sorted(set(topo.chip(c) for c in T.cores))
+    nch = len(chips)
+    ci = chips.index(topo.chip(core))
+    sib = [c for c in T.cores if topo.chip(c) == topo.chip(core) and c != core][0]
+    same_die = {}
+    for c in T.cores:
+        if topo.die(c) == topo.die(core):
+            same_die[chips.index(topo.chip(c))] = c
+    dests = [same_die[(ci + s) % nch] for s in range(1, nch)]
+    for d in dests:
+        assert topo.may_write(core, d)
+    m_off = topo.mask(core, dests[0])
+    m_on = topo.mask(core, sib)
+    m_stay = (m_on & ~m_off) or m_on
+
+    def slot(lo, hi=None):
+        hi = lo if hi is None else hi
+        return T.kv[:, lo * W:(hi + 1) * W]
+
+    def kblk(s):
+        return T.kv[:, s * W:s * W + 128]
+
+    def vblk(s):
+        return T.kv[:, s * W + 128:(s + 1) * W]
+
+    sy.dma_start(kblk(0), T.k[:]).then_inc(sem.ld, 16)
+    sc.dma_start(vblk(0), T.v[:]).then_inc(sem.ld, 16)
+    sy.dma_start(T.qs[:], T.q[:]).then_inc(sem.ldq, 16)
+
+    ve.memset(T.ida[:, 1:129], 0.0).then_inc(sem.vi, 1)
+    ve.memset(T.ida[:, 0:1], 1.0).then_inc(sem.vi, 1)
+    ve.memset(T.ones[:], 1.0).then_inc(sem.vc, 1)
+    ve.memset(T.half[0:1, :], 0.5).then_inc(sem.vc, 1)
+    ve.memset(T.negh[0:1, :], -0.5).then_inc(sem.vc, 1)
+    sc.wait_ge(sem.vi, 2)
+    sc.dma_start(T.idd[:], T.ida[:]).then_inc(sem.di, 16)
+    sc.wait_ge(sem.di, 16)
+    sc.dma_start(T.ident[:], T.idd[0:128, :]).then_inc(sem.di2, 16)
+
+    sent = 0
+    g.wait_ge(sem.ld, 32)
+    ids = []
+    for d in dests:
+        rid, pid, _ = topo.addr(d)
+        ids.append(DstId(rid=rid, pnc=pid))
+    g.remote_dma_fused([RemoteDMATransfer(dst_ids=ids, dma_engine_mask=m_off, remote_sem=sem["a%d" % ci],
+                                          srcs=[slot(0)], dsts=[slot(s) for s in range(1, nch)], alu_op=0)],
+                       local_sem=sem.sent)
+    sent += _bits(m_off)
+    srid, spid, _ = topo.addr(sib)
+    fcount = []
+    for b, batch in enumerate(BATCHES):
+        for s in batch:
+            if s > 0:
+                g.wait_ge(sem["a%d" % ((ci - s) % nch)], _bits(m_off))
+        m = m_on if b == len(BATCHES) - 1 else m_stay
+        g.remote_dma(slot(8 + batch[0], 8 + batch[-1]), slot(batch[0], batch[-1]), sem["f%d" % b], sem.sent,
+                     spid, srid, m)
+        sent += _bits(m)
+        fcount.append(_bits(m))
+    g.wait_ge(sem.sent, sent)
+
+    order = []
+    for b, batch in enumerate(BATCHES):
+        order += [(s, None) for s in batch]
+        order += [(8 + s, b) for s in batch]
+
+    pT = [T.pT0, T.pT1, T.pT2]
+    pS = [T.pS0, T.pS1]
+
+    def sblk(i):
+        return pS[i // 8][:, (i % 8) * QP:(i % 8 + 1) * QP]
+
+    te.wait_ge(sem.ldq, 16)
+    te.wait_ge(sem.vc, 3)
+    for i, (s, b) in enumerate(order):
+        if s == 0:
+            te.wait_ge(sem.ld, 32)
+        elif b is None:
+            te.wait_ge(sem["a%d" % ((ci - s) % nch)], _bits(m_off))
+        else:
+            te.wait_ge(sem["f%d" % b], fcount[b])
+        if i >= NT:
+            te.wait_ge(sem.vacc, 2 * (i - NT + 1))
+        te.matmul(pT[i % NT][0:QP, 0:128], T.qs[:], kblk(s), True, True).then_inc(sem.st, 1)
+        te.matmul(sblk(i), kblk(s), T.qs[:], True, True).then_inc(sem.ss, 1)
+        mm = te.matmul(T.pV[0:1, 0:128], T.ones[:, 0:1], vblk(s), i == 0, i == NB - 1)
+        if i == NB - 1:
+            mm.then_inc(sem.sv, 1)
+    te.wait_ge(sem.di2, 16)
+    te.wait_ge(sem.vm, 1)
+    te.matmul(T.pT0[0:1, 0:QP], T.mcol[0:QP, 0:1], T.ident[0:QP, 0:QP], True, True).then_inc(sem.sm, 1)
+    te.wait_ge(sem.vrow, 1)
+    te.matmul(T.pT1[:, 0:QP], T.half[0:1, :], T.mrow[0:1, :], True, True).then_inc(sem.sh, 1)
+    te.wait_ge(sem.vx, 2)
+    te.matmul(T.pY[:, 0:QP], T.vsrow[0:1, :], T.nhrow[0:1, :], True, False)
+    for i, (s, b) in enumerate(order):
+        te.wait_ge(sem.sp, i + 1)
+        mm = te.matmul(T.pY[:, 0:QP], vblk(s), T.pp[:, i * QP:(i + 1) * QP], False, i == NB - 1)
+        if i == NB - 1:
+            mm.then_inc(sem.sy, 1)
+
+    nv = 0
+    acc = T.acc
+    for i in range(NB):
+        ve.wait_ge(sem.st, i + 1)
+        bank = pT[i % NT]
+        if i == 0:
+            ve.tensor_copy(acc[0:QP, :], bank[0:QP, 0:64]).then_inc(sem.vacc, 1)
+        else:
+            ve.wait_ge(sem.vacc, nv)
+            ve.tensor_tensor(acc[0:QP, :], bank[0:QP, 0:64], acc[0:QP, :], AluOpType.max).then_inc(sem.vacc, 1)
+        nv += 1
+        ve.wait_ge(sem.vacc, nv)
+        ve.tensor_tensor(acc[0:QP, :], bank[0:QP, 64:128], acc[0:QP, :], AluOpType.max).then_inc(sem.vacc, 1)
+        nv += 1
+    w = 32
+    while w >= 1:
+        ve.wait_ge(sem.vacc, nv)
+        if w > 1:
+            ve.tensor_tensor(acc[0:QP, 0:w], acc[0:QP, 0:w], acc[0:QP, w:2 * w], AluOpType.max).then_inc(sem.vacc, 1)
+            nv += 1
+        else:
+            ve.tensor_tensor(T.mcol[0:QP, 0:1], acc[0:QP, 0:1], acc[0:QP, 1:2], AluOpType.max).then_inc(sem.vm, 1)
+        w //= 2
+    ve.wait_ge(sem.sv, 1)
+    ve.tensor_copy(T.vsrow[0:1, :], T.pV[0:1, 0:128]).then_inc(sem.vx, 1)
+    ve.wait_ge(sem.sm, 1)
+    ve.tensor_copy(T.mrow[0:1, :], T.pT0[0:1, 0:QP]).then_inc(sem.vrow, 1)
+    ve.wait_ge(sem.vc, 3)
+    ve.tensor_tensor(T.nhrow[0:1, :], T.pT0[0:1, 0:QP], T.negh[0:1, :], AluOpType.mult).then_inc(sem.vx, 1)
+    ve.wait_ge(sem.sh, 1)
+    ve.tensor_copy(T.hb[:], T.pT1[:, 0:QP]).then_inc(sem.vh, 1)
+    ve.wait_ge(sem.vh, 1)
+    ve.wait_ge(sem.ss, NB)
+    for i in range(NB):
+        ve.tensor_tensor(T.pp[:, i * QP:(i + 1) * QP], sblk(i), T.hb[:], AluOpType.max).then_inc(sem.sp, 1)
+    ve.wait_ge(sem.sy, 1)
+    ve.tensor_copy(T.ysb[:], T.pY[:, 0:QP]).then_inc(sem.vy, 1)
+
+    sy.wait_ge(sem.vy, 1)
+    sy.dma_start(T.y[:], T.ysb[:]).then_inc(sem.sto, 16)
+    sy.wait_ge(sem.sto, 16)

@@ -4,20 +4,24 @@ from concourse.mybir import AluOpType
 NB = 16
 W = 256
 QP = 64
+WAVES = [[1, 2], [3, 4], [5, 6], [7]]
 BATCHES = [[0], [1, 2], [3, 4], [5, 6], [7]]
-NT = 3
+NT = 4
+LATE = 6
+HOP = 24
 
 SCRATCH = {
     "kv": ("sbuf", [128, NB * W], "bfloat16"),
-    "qs": ("sbuf", [128, QP], "bfloat16"),
+    "qz": ("sbuf", [128, 3 * QP], "bfloat16"),
     "ida": ("sbuf", [128, 129], "bfloat16"),
     "idd": ("dram", [129, 128], "bfloat16"),
     "ident": ("sbuf", [128, 128], "bfloat16"),
     "ones": ("sbuf", [128, 8], "bfloat16"),
     "half": ("sbuf", [128, 128], "bfloat16"),
-    "negh": ("sbuf", [128, QP], "float32"),
-    "acc": ("sbuf", [128, QP], "float32"),
+    "negh": ("sbuf", [128, QP], "bfloat16"),
+    "acc": ("sbuf", [128, 128], "float32"),
     "mcol": ("sbuf", [128, 8], "bfloat16"),
+    "r1": ("sbuf", [128, QP], "float32"),
     "mrow": ("sbuf", [128, QP], "bfloat16"),
     "nhrow": ("sbuf", [128, QP], "float32"),
     "vsrow": ("sbuf", [128, 128], "float32"),
@@ -29,12 +33,13 @@ SCRATCH = {
     "pT0": ("psum", [128, 512], "float32"),
     "pT1": ("psum", [128, 512], "float32"),
     "pT2": ("psum", [128, 512], "float32"),
+    "pT3": ("psum", [128, 512], "float32"),
     "pV": ("psum", [128, 512], "float32"),
     "pY": ("psum", [128, 512], "float32"),
 }
-SEMAPHORES = (["a%d" % i for i in range(8)] + ["f%d" % i for i in range(len(BATCHES))] +
-              ["ld", "ldq", "vi", "di", "di2", "vc", "st", "ss", "sv", "vacc", "vm", "sm", "vrow", "vx", "sh", "vh",
-               "sp", "sy", "vy", "sto", "sent"])
+SEMAPHORES = (["a%d" % i for i in range(16)] + ["f%d" % i for i in range(len(BATCHES))] +
+              ["ld", "ldq", "vi", "di", "di2", "vc", "st", "ss", "sv", "vacc", "vm", "sm", "vr", "vrow", "vx", "sh",
+               "vh", "sp", "sy", "vy", "sto", "sent"])
 
 
 def _bits(m):
@@ -55,12 +60,22 @@ def rank_program(g, core, T, topo):
     for c in T.cores:
         if topo.die(c) == topo.die(core):
             same_die[chips.index(topo.chip(c))] = c
-    dests = [same_die[(ci + s) % nch] for s in range(1, nch)]
-    for d in dests:
-        assert topo.may_write(core, d)
-    m_off = topo.mask(core, dests[0])
+    dest = {}
+    for s in range(1, nch):
+        dest[s] = same_die[(ci + s) % nch]
+        assert topo.may_write(core, dest[s])
+    m_off = topo.mask(core, dest[1])
     m_on = topo.mask(core, sib)
     m_stay = (m_on & ~m_off) or m_on
+    eng = [e for e in range(32) if (m_off >> e) & 1]
+    smask = {}
+    for wave in WAVES:
+        per = len(eng) // len(wave)
+        for j, s in enumerate(wave):
+            smask[s] = sum(1 << e for e in eng[j * per:(j + 1) * per])
+
+    def asem(s):
+        return sem["a%d" % T.rank_of(same_die[(ci - s) % nch])]
 
     def slot(lo, hi=None):
         hi = lo if hi is None else hi
@@ -72,12 +87,19 @@ def rank_program(g, core, T, topo):
     def vblk(s):
         return T.kv[:, s * W + 128:(s + 1) * W]
 
+    q = T.qz[:, QP:2 * QP]
+    q_lo = T.qz[:, QP:3 * QP]
+    q_hi = T.qz[:, 0:2 * QP]
+
     sy.dma_start(kblk(0), T.k[:]).then_inc(sem.ld, 16)
     sc.dma_start(vblk(0), T.v[:]).then_inc(sem.ld, 16)
-    sy.dma_start(T.qs[:], T.q[:]).then_inc(sem.ldq, 16)
+    sy.dma_start(q, T.q[:]).then_inc(sem.ldq, 16)
 
+    NC = 5
     ve.memset(T.ida[:, 1:129], 0.0).then_inc(sem.vi, 1)
     ve.memset(T.ida[:, 0:1], 1.0).then_inc(sem.vi, 1)
+    ve.memset(T.qz[:, 0:QP], 0.0).then_inc(sem.vc, 1)
+    ve.memset(T.qz[:, 2 * QP:3 * QP], 0.0).then_inc(sem.vc, 1)
     ve.memset(T.ones[:], 1.0).then_inc(sem.vc, 1)
     ve.memset(T.half[0:1, :], 0.5).then_inc(sem.vc, 1)
     ve.memset(T.negh[0:1, :], -0.5).then_inc(sem.vc, 1)
@@ -88,20 +110,21 @@ def rank_program(g, core, T, topo):
 
     sent = 0
     g.wait_ge(sem.ld, 32)
-    ids = []
-    for d in dests:
-        rid, pid, _ = topo.addr(d)
-        ids.append(DstId(rid=rid, pnc=pid))
-    g.remote_dma_fused([RemoteDMATransfer(dst_ids=ids, dma_engine_mask=m_off, remote_sem=sem["a%d" % ci],
-                                          srcs=[slot(0)], dsts=[slot(s) for s in range(1, nch)], alu_op=0)],
-                       local_sem=sem.sent)
-    sent += _bits(m_off)
+    for wave in WAVES:
+        trs = []
+        for s in wave:
+            rid, pid, _ = topo.addr(dest[s])
+            trs.append(RemoteDMATransfer(dst_ids=[DstId(rid=rid, pnc=pid)], dma_engine_mask=smask[s],
+                                         remote_sem=sem["a%d" % T.rank_of(core)], srcs=[slot(0)], dsts=[slot(s)],
+                                         alu_op=0))
+            sent += _bits(smask[s])
+        g.remote_dma_fused(trs, local_sem=sem.sent)
     srid, spid, _ = topo.addr(sib)
     fcount = []
     for b, batch in enumerate(BATCHES):
         for s in batch:
             if s > 0:
-                g.wait_ge(sem["a%d" % ((ci - s) % nch)], _bits(m_off))
+                g.wait_ge(asem(s), _bits(smask[s]))
         m = m_on if b == len(BATCHES) - 1 else m_stay
         g.remote_dma(slot(8 + batch[0], 8 + batch[-1]), slot(batch[0], batch[-1]), sem["f%d" % b], sem.sent,
                      spid, srid, m)
@@ -109,36 +132,52 @@ def rank_program(g, core, T, topo):
         fcount.append(_bits(m))
     g.wait_ge(sem.sent, sent)
 
-    order = []
+    est = {0: (0, None)}
+    t = 0
+    for wave in WAVES:
+        t += 16 * len(wave)
+        for s in wave:
+            est[s] = (t, None)
     for b, batch in enumerate(BATCHES):
-        order += [(s, None) for s in batch]
-        order += [(8 + s, b) for s in batch]
+        t = max(est[s][0] for s in batch) + HOP + 16 * len(batch) - (40 if b == 0 else 0)
+        for s in batch:
+            est[8 + s] = (t, b)
+    order = [(s, est[s][1]) for s in sorted(est, key=lambda x: (est[x][0], x))]
 
-    pT = [T.pT0, T.pT1, T.pT2]
+    pT = [T.pT0, T.pT1, T.pT2, T.pT3]
     pS = [T.pS0, T.pS1]
 
     def sblk(i):
         return pS[i // 8][:, (i % 8) * QP:(i % 8 + 1) * QP]
 
     te.wait_ge(sem.ldq, 16)
-    te.wait_ge(sem.vc, 3)
+    te.wait_ge(sem.vc, NC)
     for i, (s, b) in enumerate(order):
         if s == 0:
             te.wait_ge(sem.ld, 32)
         elif b is None:
-            te.wait_ge(sem["a%d" % ((ci - s) % nch)], _bits(m_off))
+            te.wait_ge(asem(s), _bits(smask[s]))
         else:
             te.wait_ge(sem["f%d" % b], fcount[b])
-        if i >= NT:
-            te.wait_ge(sem.vacc, 2 * (i - NT + 1))
-        te.matmul(pT[i % NT][0:QP, 0:128], T.qs[:], kblk(s), True, True).then_inc(sem.st, 1)
-        te.matmul(sblk(i), kblk(s), T.qs[:], True, True).then_inc(sem.ss, 1)
-        mm = te.matmul(T.pV[0:1, 0:128], T.ones[:, 0:1], vblk(s), i == 0, i == NB - 1)
+        p = i // 2
+        if i % 2 == 0:
+            if p >= NT:
+                te.wait_ge(sem.vacc, p - NT + 1)
+            te.matmul(pT[p % NT][:, 0:128], q_lo, kblk(s), True, False)
+        else:
+            te.matmul(pT[p % NT][:, 0:128], q_hi, kblk(s), False, True).then_inc(sem.st, 1)
+        if i < NB - LATE:
+            te.matmul(sblk(i), kblk(s), q, True, True).then_inc(sem.ss, 1)
+            te.matmul(T.pV[0:1, 0:128], T.ones[:, 0:1], vblk(s), i == 0, False)
+    for i in range(NB - LATE, NB):
+        te.matmul(sblk(i), kblk(order[i][0]), q, True, True).then_inc(sem.ss, 1)
+    for i in range(NB - LATE, NB):
+        mm = te.matmul(T.pV[0:1, 0:128], T.ones[:, 0:1], vblk(order[i][0]), False, i == NB - 1)
         if i == NB - 1:
             mm.then_inc(sem.sv, 1)
     te.wait_ge(sem.di2, 16)
     te.wait_ge(sem.vm, 1)
-    te.matmul(T.pT0[0:1, 0:QP], T.mcol[0:QP, 0:1], T.ident[0:QP, 0:QP], True, True).then_inc(sem.sm, 1)
+    te.matmul(T.pT0[0:1, 0:128], T.mcol[:, 0:1], T.ident[:], True, True).then_inc(sem.sm, 1)
     te.wait_ge(sem.vrow, 1)
     te.matmul(T.pT1[:, 0:QP], T.half[0:1, :], T.mrow[0:1, :], True, True).then_inc(sem.sh, 1)
     te.wait_ge(sem.vx, 2)
@@ -151,33 +190,33 @@ def rank_program(g, core, T, topo):
 
     nv = 0
     acc = T.acc
-    for i in range(NB):
-        ve.wait_ge(sem.st, i + 1)
-        bank = pT[i % NT]
-        if i == 0:
-            ve.tensor_copy(acc[0:QP, :], bank[0:QP, 0:64]).then_inc(sem.vacc, 1)
+    for p in range(NB // 2):
+        ve.wait_ge(sem.st, p + 1)
+        bank = pT[p % NT]
+        if p == 0:
+            ve.tensor_copy(acc[:], bank[:, 0:128]).then_inc(sem.vacc, 1)
         else:
             ve.wait_ge(sem.vacc, nv)
-            ve.tensor_tensor(acc[0:QP, :], bank[0:QP, 0:64], acc[0:QP, :], AluOpType.max).then_inc(sem.vacc, 1)
+            ve.tensor_tensor(acc[:], bank[:, 0:128], acc[:], AluOpType.max).then_inc(sem.vacc, 1)
         nv += 1
-        ve.wait_ge(sem.vacc, nv)
-        ve.tensor_tensor(acc[0:QP, :], bank[0:QP, 64:128], acc[0:QP, :], AluOpType.max).then_inc(sem.vacc, 1)
-        nv += 1
-    w = 32
+    w = 64
     while w >= 1:
         ve.wait_ge(sem.vacc, nv)
         if w > 1:
-            ve.tensor_tensor(acc[0:QP, 0:w], acc[0:QP, 0:w], acc[0:QP, w:2 * w], AluOpType.max).then_inc(sem.vacc, 1)
+            ve.tensor_tensor(acc[:, 0:w], acc[:, 0:w], acc[:, w:2 * w], AluOpType.max).then_inc(sem.vacc, 1)
             nv += 1
         else:
-            ve.tensor_tensor(T.mcol[0:QP, 0:1], acc[0:QP, 0:1], acc[0:QP, 1:2], AluOpType.max).then_inc(sem.vm, 1)
+            ve.tensor_tensor(T.mcol[:, 0:1], acc[:, 0:1], acc[:, 1:2], AluOpType.max).then_inc(sem.vm, 1)
         w //= 2
     ve.wait_ge(sem.sv, 1)
     ve.tensor_copy(T.vsrow[0:1, :], T.pV[0:1, 0:128]).then_inc(sem.vx, 1)
     ve.wait_ge(sem.sm, 1)
-    ve.tensor_copy(T.mrow[0:1, :], T.pT0[0:1, 0:QP]).then_inc(sem.vrow, 1)
-    ve.wait_ge(sem.vc, 3)
-    ve.tensor_tensor(T.nhrow[0:1, :], T.pT0[0:1, 0:QP], T.negh[0:1, :], AluOpType.mult).then_inc(sem.vx, 1)
+    ve.tensor_copy(T.r1[0:1, :], T.pT0[0:1, QP:2 * QP]).then_inc(sem.vr, 1)
+    ve.wait_ge(sem.vr, 1)
+    ve.tensor_tensor(T.mrow[0:1, :], T.pT0[0:1, 0:QP], T.r1[0:1, :], AluOpType.max).then_inc(sem.vrow, 1)
+    ve.wait_ge(sem.vrow, 1)
+    ve.wait_ge(sem.vc, NC)
+    ve.tensor_tensor(T.nhrow[0:1, :], T.mrow[0:1, :], T.negh[0:1, :], AluOpType.mult).then_inc(sem.vx, 1)
     ve.wait_ge(sem.sh, 1)
     ve.tensor_copy(T.hb[:], T.pT1[:, 0:QP]).then_inc(sem.vh, 1)
     ve.wait_ge(sem.vh, 1)

@@ -1,32 +1,32 @@
 from concourse.bass import DstId, RemoteDMATransfer
-from concourse.mybir import AluOpType
+from concourse.mybir import AluOpType, AxisListType
 
 NB = 16
-W = 256
+W = 128
 QP = 64
+PW = 72
+PN = 66
 WAVES = [[1, 2], [3, 4], [5, 6], [7]]
 BATCHES = [[0], [1, 2], [3, 4], [5, 6], [7]]
 NT = 4
-LATE = 6
+SOLO = 2
 HOP = 24
 
 SCRATCH = {
-    "kv": ("sbuf", [128, NB * W], "bfloat16"),
-    "qz": ("sbuf", [128, 3 * QP], "bfloat16"),
+    "kk": ("sbuf", [128, NB * W], "bfloat16"),
+    "vv": ("sbuf", [128, NB * W], "bfloat16"),
+    "qq": ("sbuf", [128, QP], "bfloat16"),
     "ida": ("sbuf", [128, 129], "bfloat16"),
     "idd": ("dram", [129, 128], "bfloat16"),
     "ident": ("sbuf", [128, 128], "bfloat16"),
-    "ones": ("sbuf", [128, 8], "bfloat16"),
     "half": ("sbuf", [128, 128], "bfloat16"),
-    "negh": ("sbuf", [128, QP], "bfloat16"),
-    "acc": ("sbuf", [128, 128], "float32"),
-    "mcol": ("sbuf", [128, 8], "bfloat16"),
-    "r1": ("sbuf", [128, QP], "float32"),
-    "mrow": ("sbuf", [128, QP], "bfloat16"),
-    "nhrow": ("sbuf", [128, QP], "float32"),
-    "vsrow": ("sbuf", [128, 128], "float32"),
+    "acc": ("sbuf", [128, 2 * QP], "float32"),
+    "accb": ("sbuf", [128, QP], "bfloat16"),
+    "mcol": ("sbuf", [128, 8], "float32"),
+    "diag": ("sbuf", [128, QP], "bfloat16"),
     "hb": ("sbuf", [128, QP], "bfloat16"),
-    "pp": ("sbuf", [128, NB * QP], "bfloat16"),
+    "cc": ("sbuf", [128, QP], "float32"),
+    "pp": ("sbuf", [128, NB * PW], "bfloat16"),
     "ysb": ("sbuf", [128, QP], "bfloat16"),
     "pS0": ("psum", [128, 512], "float32"),
     "pS1": ("psum", [128, 512], "float32"),
@@ -34,91 +34,170 @@ SCRATCH = {
     "pT1": ("psum", [128, 512], "float32"),
     "pT2": ("psum", [128, 512], "float32"),
     "pT3": ("psum", [128, 512], "float32"),
-    "pV": ("psum", [128, 512], "float32"),
+    "pH": ("psum", [128, 512], "float32"),
     "pY": ("psum", [128, 512], "float32"),
 }
-SEMAPHORES = (["a%d" % i for i in range(16)] + ["f%d" % i for i in range(len(BATCHES))] +
-              ["ld", "ldq", "vi", "di", "di2", "vc", "st", "ss", "sv", "vacc", "vm", "sm", "vr", "vrow", "vx", "sh",
-               "vh", "sp", "sy", "vy", "sto", "sent"])
+SEMAPHORES = (["a%d" % i for i in range(NB)] + ["b%d" % i for i in range(NB)] + ["c%d" % i for i in range(NB)] +
+              ["f%d" % i for i in range(len(BATCHES))] +
+              ["hv", "ldk", "ldv", "ldq", "vi", "di", "di2", "vc", "st", "ss", "vacc", "vm", "sm", "vr", "vd", "sh",
+               "vh", "sp", "sy", "vq", "vy", "sto", "sent"])
 
 
 def _bits(m):
     return bin(m).count("1")
 
 
+def _split(mask, n):
+    eng = [e for e in range(32) if (mask >> e) & 1]
+    per = len(eng) // n
+    return [sum(1 << e for e in eng[j * per:(j + 1) * per]) for j in range(n)]
+
+
 def rank_program(g, core, T, topo):
-    if T.rank_of(core) is None:
-        return
     sem = T.sem
     te, ve, sy, sc = g.tensor, g.vector, g.sync, g.scalar
 
     chips = sorted(set(topo.chip(c) for c in T.cores))
+    if topo.chip(core) not in chips:
+        return
     nch = len(chips)
     ci = chips.index(topo.chip(core))
-    sib = [c for c in T.cores if topo.chip(c) == topo.chip(core) and c != core][0]
-    same_die = {}
-    for c in T.cores:
-        if topo.die(c) == topo.die(core):
-            same_die[chips.index(topo.chip(c))] = c
+    d = topo.die(core)
+    od = [topo.die(c) for c in T.cores if topo.chip(c) == topo.chip(core) and topo.die(c) != d][0]
+    everyone = range(topo.CHIPS * topo.CORES_PER_CHIP)
+
+    def rank_at(i, dd):
+        return [c for c in T.cores if topo.chip(c) == chips[i] and topo.die(c) == dd][0]
+
+    def helpers(i, dd):
+        cand = [c for c in everyone if topo.chip(c) == chips[i] and topo.die(c) == dd and T.rank_of(c) is None]
+        cand.sort(key=lambda h: (-sum(1 for c in T.cores if topo.may_write(h, c)), h))
+        return cand[:2]
+
+    def recv(i, s, dd):
+        return helpers((i + s) % nch, dd)[s % 2]
+
+    def vplan(i, dd):
+        hl = helpers(i, dd)
+        load = dict((h, []) for h in hl)
+        can = dict((s, [h for h in hl if topo.may_write(h, recv(i, s, dd))]) for s in range(1, nch))
+        for s in sorted(can, key=lambda x: (len(can[x]), x)):
+            h = min(can[s], key=lambda x: (len(load[x]), -hl.index(x)))
+            load[h].append(s)
+        plan = {}
+        for h in hl:
+            steps = sorted(load[h])
+            for w in range(0, len(steps), 2):
+                wave = steps[w:w + 2]
+                ms = _split(topo.mask(h, recv(i, wave[0], dd)), len(wave))
+                for j, s in enumerate(wave):
+                    plan[s] = (h, w // 2, ms[j])
+        return plan
+
+    def kblk(lo, hi=None):
+        hi = lo if hi is None else hi
+        return T.kk[:, lo * W:(hi + 1) * W]
+
+    def vblk(r):
+        return T.vv[:, r * W:(r + 1) * W]
+
+    def transfer(dst, mask, rsem, src_ap, dst_ap):
+        rid, pid, _ = topo.addr(dst)
+        return RemoteDMATransfer(dst_ids=[DstId(rid=rid, pnc=pid)], dma_engine_mask=mask, remote_sem=rsem,
+                                 srcs=[src_ap], dsts=[dst_ap], alu_op=0)
+
+    def stay(a, on_chip, off_chip):
+        m_on = topo.mask(a, on_chip)
+        return (m_on & ~topo.mask(a, off_chip)) or m_on
+
+    if T.rank_of(core) is None:
+        hl = helpers(ci, d)
+        if core not in hl:
+            return
+        mine, other = rank_at(ci, d), rank_at(ci, od)
+        r0 = T.rank_of(mine)
+        sent = 0
+        g.wait_ge(sem.hv, _bits(_split(stay(mine, core, rank_at((ci + 1) % nch, d)), 2)[0]))
+        waves = {}
+        for s, (h, w, m) in vplan(ci, d).items():
+            if h == core:
+                waves.setdefault(w, []).append((s, m))
+        for w in sorted(waves):
+            trs = []
+            for s, m in sorted(waves[w]):
+                trs.append(transfer(recv(ci, s, d), m, sem["c%d" % r0], vblk(r0), vblk(r0)))
+                sent += _bits(m)
+            g.remote_dma_fused(trs, local_sem=sem.sent)
+        if hl.index(core) == 1:
+            m = stay(core, other, recv(ci, 1, d))
+            rid, pid, _ = topo.addr(other)
+            g.remote_dma(vblk(r0), vblk(r0), sem["b%d" % r0], sem.sent, pid, rid, m)
+            sent += _bits(m)
+        inc = []
+        for s in range(1, nch):
+            cs = (ci - s) % nch
+            if recv(cs, s, d) == core:
+                h, w, m = vplan(cs, d)[s]
+                inc.append((w, s, T.rank_of(rank_at(cs, d)), _bits(m)))
+        lo, hi = _split(topo.mask(core, other), 2)
+        for w, s, r, n in sorted(inc):
+            g.wait_ge(sem["c%d" % r], n)
+            g.remote_dma_fused([transfer(mine, lo, sem["b%d" % r], vblk(r), vblk(r)),
+                                transfer(other, hi, sem["b%d" % r], vblk(r), vblk(r))], local_sem=sem.sent)
+            sent += _bits(lo) + _bits(hi)
+        g.wait_ge(sem.sent, sent)
+        return
+
+    me = T.rank_of(core)
+    sib = rank_at(ci, od)
     dest = {}
     for s in range(1, nch):
-        dest[s] = same_die[(ci + s) % nch]
+        dest[s] = rank_at((ci + s) % nch, d)
         assert topo.may_write(core, dest[s])
     m_off = topo.mask(core, dest[1])
     m_on = topo.mask(core, sib)
-    m_stay = (m_on & ~m_off) or m_on
-    eng = [e for e in range(32) if (m_off >> e) & 1]
+    m_stay = stay(core, sib, dest[1])
     smask = {}
     for wave in WAVES:
-        per = len(eng) // len(wave)
-        for j, s in enumerate(wave):
-            smask[s] = sum(1 << e for e in eng[j * per:(j + 1) * per])
+        for s, m in zip(wave, _split(m_off, len(wave))):
+            smask[s] = m
 
     def asem(s):
-        return sem["a%d" % T.rank_of(same_die[(ci - s) % nch])]
+        return sem["a%d" % T.rank_of(rank_at((ci - s) % nch, d))]
 
-    def slot(lo, hi=None):
-        hi = lo if hi is None else hi
-        return T.kv[:, lo * W:(hi + 1) * W]
+    def slot_rank(s):
+        return T.rank_of(rank_at((ci - s) % nch, d)) if s < nch else T.rank_of(rank_at((ci - s) % nch, od))
 
-    def kblk(s):
-        return T.kv[:, s * W:s * W + 128]
+    q = T.qq[:]
 
-    def vblk(s):
-        return T.kv[:, s * W + 128:(s + 1) * W]
-
-    q = T.qz[:, QP:2 * QP]
-    q_lo = T.qz[:, QP:3 * QP]
-    q_hi = T.qz[:, 0:2 * QP]
-
-    sy.dma_start(kblk(0), T.k[:]).then_inc(sem.ld, 16)
-    sc.dma_start(vblk(0), T.v[:]).then_inc(sem.ld, 16)
+    sy.dma_start(kblk(0), T.k[:]).then_inc(sem.ldk, 16)
+    sc.dma_start(vblk(me), T.v[:]).then_inc(sem.ldv, 16)
     sy.dma_start(q, T.q[:]).then_inc(sem.ldq, 16)
 
-    NC = 5
+    NC = 2
     ve.memset(T.ida[:, 1:129], 0.0).then_inc(sem.vi, 1)
     ve.memset(T.ida[:, 0:1], 1.0).then_inc(sem.vi, 1)
-    ve.memset(T.qz[:, 0:QP], 0.0).then_inc(sem.vc, 1)
-    ve.memset(T.qz[:, 2 * QP:3 * QP], 0.0).then_inc(sem.vc, 1)
-    ve.memset(T.ones[:], 1.0).then_inc(sem.vc, 1)
-    ve.memset(T.half[0:1, :], 0.5).then_inc(sem.vc, 1)
-    ve.memset(T.negh[0:1, :], -0.5).then_inc(sem.vc, 1)
+    ve.memset(T.half[:], 0.5).then_inc(sem.vc, 1)
+    ve.memset(T.pp[:], 1.0).then_inc(sem.vc, 1)
     sc.wait_ge(sem.vi, 2)
     sc.dma_start(T.idd[:], T.ida[:]).then_inc(sem.di, 16)
     sc.wait_ge(sem.di, 16)
     sc.dma_start(T.ident[:], T.idd[0:128, :]).then_inc(sem.di2, 16)
 
     sent = 0
-    g.wait_ge(sem.ld, 32)
+    g.wait_ge(sem.ldk, 16)
     for wave in WAVES:
         trs = []
         for s in wave:
-            rid, pid, _ = topo.addr(dest[s])
-            trs.append(RemoteDMATransfer(dst_ids=[DstId(rid=rid, pnc=pid)], dma_engine_mask=smask[s],
-                                         remote_sem=sem["a%d" % T.rank_of(core)], srcs=[slot(0)], dsts=[slot(s)],
-                                         alu_op=0))
+            trs.append(transfer(dest[s], smask[s], sem["a%d" % me], kblk(0), kblk(s)))
             sent += _bits(smask[s])
         g.remote_dma_fused(trs, local_sem=sem.sent)
+    g.wait_ge(sem.ldv, 16)
+    trs = []
+    for h, m in zip(helpers(ci, d), _split(m_stay, 2)):
+        trs.append(transfer(h, m, sem.hv, vblk(me), vblk(me)))
+        sent += _bits(m)
+    g.remote_dma_fused(trs, local_sem=sem.sent)
     srid, spid, _ = topo.addr(sib)
     fcount = []
     for b, batch in enumerate(BATCHES):
@@ -126,7 +205,7 @@ def rank_program(g, core, T, topo):
             if s > 0:
                 g.wait_ge(asem(s), _bits(smask[s]))
         m = m_on if b == len(BATCHES) - 1 else m_stay
-        g.remote_dma(slot(8 + batch[0], 8 + batch[-1]), slot(batch[0], batch[-1]), sem["f%d" % b], sem.sent,
+        g.remote_dma(kblk(nch + batch[0], nch + batch[-1]), kblk(batch[0], batch[-1]), sem["f%d" % b], sem.sent,
                      spid, srid, m)
         sent += _bits(m)
         fcount.append(_bits(m))
@@ -141,7 +220,7 @@ def rank_program(g, core, T, topo):
     for b, batch in enumerate(BATCHES):
         t = max(est[s][0] for s in batch) + HOP + 16 * len(batch) - (40 if b == 0 else 0)
         for s in batch:
-            est[8 + s] = (t, b)
+            est[nch + s] = (t, b)
     order = [(s, est[s][1]) for s in sorted(est, key=lambda x: (est[x][0], x))]
 
     pT = [T.pT0, T.pT1, T.pT2, T.pT3]
@@ -150,81 +229,82 @@ def rank_program(g, core, T, topo):
     def sblk(i):
         return pS[i // 8][:, (i % 8) * QP:(i % 8 + 1) * QP]
 
+    units = [[i, i + 1] for i in range(0, NB - SOLO, 2)] + [[i] for i in range(NB - SOLO, NB)]
+    npair = (NB - SOLO) // 2
+
     te.wait_ge(sem.ldq, 16)
-    te.wait_ge(sem.vc, NC)
-    for i, (s, b) in enumerate(order):
-        if s == 0:
-            te.wait_ge(sem.ld, 32)
-        elif b is None:
-            te.wait_ge(asem(s), _bits(smask[s]))
-        else:
-            te.wait_ge(sem["f%d" % b], fcount[b])
-        p = i // 2
-        if i % 2 == 0:
-            if p >= NT:
-                te.wait_ge(sem.vacc, p - NT + 1)
-            te.matmul(pT[p % NT][:, 0:128], q_lo, kblk(s), True, False)
-        else:
-            te.matmul(pT[p % NT][:, 0:128], q_hi, kblk(s), False, True).then_inc(sem.st, 1)
-        if i < NB - LATE:
+    for u, unit in enumerate(units):
+        for j, i in enumerate(unit):
+            s, b = order[i]
+            if s == 0:
+                te.wait_ge(sem.ldk, 16)
+            elif b is None:
+                te.wait_ge(asem(s), _bits(smask[s]))
+            else:
+                te.wait_ge(sem["f%d" % b], fcount[b])
+            if j == 0 and u >= NT:
+                te.wait_ge(sem.vacc, u - NT + 1)
+            mm = te.matmul(pT[u % NT][:, j * QP:(j + 1) * QP], kblk(s), q, True, True)
+            if j == len(unit) - 1:
+                mm.then_inc(sem.st, 1)
             te.matmul(sblk(i), kblk(s), q, True, True).then_inc(sem.ss, 1)
-            te.matmul(T.pV[0:1, 0:128], T.ones[:, 0:1], vblk(s), i == 0, False)
-    for i in range(NB - LATE, NB):
-        te.matmul(sblk(i), kblk(order[i][0]), q, True, True).then_inc(sem.ss, 1)
-    for i in range(NB - LATE, NB):
-        mm = te.matmul(T.pV[0:1, 0:128], T.ones[:, 0:1], vblk(order[i][0]), False, i == NB - 1)
-        if i == NB - 1:
-            mm.then_inc(sem.sv, 1)
     te.wait_ge(sem.di2, 16)
     te.wait_ge(sem.vm, 1)
-    te.matmul(T.pT0[0:1, 0:128], T.mcol[:, 0:1], T.ident[:], True, True).then_inc(sem.sm, 1)
-    te.wait_ge(sem.vrow, 1)
-    te.matmul(T.pT1[:, 0:QP], T.half[0:1, :], T.mrow[0:1, :], True, True).then_inc(sem.sh, 1)
-    te.wait_ge(sem.vx, 2)
-    te.matmul(T.pY[:, 0:QP], T.vsrow[0:1, :], T.nhrow[0:1, :], True, False)
+    te.matmul(T.pT0[0:QP, 0:128], T.accb[:], T.ident[:], True, True).then_inc(sem.sm, 1)
+    te.wait_ge(sem.vc, NC)
+    te.wait_ge(sem.vd, 1)
+    te.matmul(T.pH[:, 0:QP], T.half[0:QP, :], T.diag[0:QP, :], True, True).then_inc(sem.sh, 1)
+    hs = helpers(ci, od)
     for i, (s, b) in enumerate(order):
+        r = slot_rank(s)
+        if r == me:
+            te.wait_ge(sem.ldv, 16)
+        elif s == nch:
+            te.wait_ge(sem["b%d" % r], _bits(stay(hs[1], core, recv(ci, 1, od))))
+        else:
+            te.wait_ge(sem["b%d" % r], _bits(_split(topo.mask(hs[0], core), 2)[0]))
         te.wait_ge(sem.sp, i + 1)
-        mm = te.matmul(T.pY[:, 0:QP], vblk(s), T.pp[:, i * QP:(i + 1) * QP], False, i == NB - 1)
+        mm = te.matmul(T.pY[:, 0:PN], vblk(r), T.pp[:, i * PW:i * PW + PN], i == 0, i == NB - 1)
         if i == NB - 1:
             mm.then_inc(sem.sy, 1)
 
-    nv = 0
     acc = T.acc
-    for p in range(NB // 2):
-        ve.wait_ge(sem.st, p + 1)
-        bank = pT[p % NT]
-        if p == 0:
-            ve.tensor_copy(acc[:], bank[:, 0:128]).then_inc(sem.vacc, 1)
-        else:
+    nv = 0
+    for u, unit in enumerate(units):
+        ve.wait_ge(sem.st, u + 1)
+        bank = pT[u % NT]
+        if nv:
             ve.wait_ge(sem.vacc, nv)
-            ve.tensor_tensor(acc[:], bank[:, 0:128], acc[:], AluOpType.max).then_inc(sem.vacc, 1)
-        nv += 1
-    w = 64
-    while w >= 1:
-        ve.wait_ge(sem.vacc, nv)
-        if w > 1:
-            ve.tensor_tensor(acc[:, 0:w], acc[:, 0:w], acc[:, w:2 * w], AluOpType.max).then_inc(sem.vacc, 1)
-            nv += 1
+        if u == 0:
+            ve.tensor_copy(acc[:], bank[:, 0:2 * QP]).then_inc(sem.vacc, 1)
+        elif u < npair:
+            ve.tensor_tensor(acc[:], bank[:, 0:2 * QP], acc[:], AluOpType.max).then_inc(sem.vacc, 1)
+        elif u < len(units) - 1:
+            ve.tensor_tensor(acc[:, 0:QP], bank[:, 0:QP], acc[:, 0:QP], AluOpType.max).then_inc(sem.vacc, 1)
         else:
-            ve.tensor_tensor(T.mcol[:, 0:1], acc[:, 0:1], acc[:, 1:2], AluOpType.max).then_inc(sem.vm, 1)
-        w //= 2
-    ve.wait_ge(sem.sv, 1)
-    ve.tensor_copy(T.vsrow[0:1, :], T.pV[0:1, 0:128]).then_inc(sem.vx, 1)
+            ve.tensor_tensor(T.accb[:], bank[:, 0:QP], acc[:, 0:QP], AluOpType.max).then_inc(sem.vm, 1)
+            break
+        nv += 1
+        if u == npair - 1:
+            ve.wait_ge(sem.vacc, nv)
+            ve.tensor_tensor(acc[:, 0:QP], acc[:, 0:QP], acc[:, QP:2 * QP], AluOpType.max).then_inc(sem.vacc, 1)
+            nv += 1
     ve.wait_ge(sem.sm, 1)
-    ve.tensor_copy(T.r1[0:1, :], T.pT0[0:1, QP:2 * QP]).then_inc(sem.vr, 1)
+    ve.tensor_reduce(T.mcol[0:QP, 0:1], T.pT0[0:QP, 0:128], AxisListType.X, AluOpType.max).then_inc(sem.vr, 1)
     ve.wait_ge(sem.vr, 1)
-    ve.tensor_tensor(T.mrow[0:1, :], T.pT0[0:1, 0:QP], T.r1[0:1, :], AluOpType.max).then_inc(sem.vrow, 1)
-    ve.wait_ge(sem.vrow, 1)
-    ve.wait_ge(sem.vc, NC)
-    ve.tensor_tensor(T.nhrow[0:1, :], T.mrow[0:1, :], T.negh[0:1, :], AluOpType.mult).then_inc(sem.vx, 1)
+    ve.wait_ge(sem.di2, 16)
+    ve.tensor_scalar(T.diag[0:QP, :], T.ident[0:QP, 0:QP], T.mcol[0:QP, 0:1], None, AluOpType.mult).then_inc(sem.vd, 1)
     ve.wait_ge(sem.sh, 1)
-    ve.tensor_copy(T.hb[:], T.pT1[:, 0:QP]).then_inc(sem.vh, 1)
+    ve.tensor_copy(T.hb[:], T.pH[:, 0:QP]).then_inc(sem.vh, 1)
     ve.wait_ge(sem.vh, 1)
+    ve.wait_ge(sem.vc, NC)
     ve.wait_ge(sem.ss, NB)
     for i in range(NB):
-        ve.tensor_tensor(T.pp[:, i * QP:(i + 1) * QP], sblk(i), T.hb[:], AluOpType.max).then_inc(sem.sp, 1)
+        ve.tensor_tensor(T.pp[:, i * PW:i * PW + QP], sblk(i), T.hb[:], AluOpType.max).then_inc(sem.sp, 1)
     ve.wait_ge(sem.sy, 1)
-    ve.tensor_copy(T.ysb[:], T.pY[:, 0:QP]).then_inc(sem.vy, 1)
+    ve.tensor_scalar(T.cc[:], T.hb[:], T.pY[:, QP:QP + 1], None, AluOpType.mult).then_inc(sem.vq, 1)
+    ve.wait_ge(sem.vq, 1)
+    ve.tensor_tensor(T.ysb[:], T.pY[:, 0:QP], T.cc[:], AluOpType.subtract).then_inc(sem.vy, 1)
 
     sy.wait_ge(sem.vy, 1)
     sy.dma_start(T.y[:], T.ysb[:]).then_inc(sem.sto, 16)

@@ -1,5 +1,5 @@
 from concourse.bass import DstId, RemoteDMATransfer
-from concourse.mybir import AluOpType, AxisListType
+from concourse.mybir import AluOpType, AxisListType, ActivationFunctionType
 
 NB = 16
 W = 128
@@ -8,7 +8,7 @@ PW = 72
 PN = 66
 WAVES = [[1, 2], [3, 4], [5, 6], [7]]
 BATCHES = [[0], [1, 2], [3, 4], [5, 6], [7]]
-NT = 4
+NT = 3
 SOLO = 2
 HOP = 24
 
@@ -20,27 +20,27 @@ SCRATCH = {
     "idd": ("dram", [129, 128], "bfloat16"),
     "ident": ("sbuf", [128, 128], "bfloat16"),
     "half": ("sbuf", [128, 128], "bfloat16"),
-    "acc": ("sbuf", [128, 2 * QP], "float32"),
-    "accb": ("sbuf", [128, QP], "bfloat16"),
-    "mcol": ("sbuf", [128, 8], "float32"),
+    "mcols": ("sbuf", [128, 16], "float32"),
+    "mfin": ("sbuf", [128, 8], "float32"),
     "diag": ("sbuf", [128, QP], "bfloat16"),
     "hb": ("sbuf", [128, QP], "bfloat16"),
     "cc": ("sbuf", [128, QP], "float32"),
+    "ssb": ("sbuf", [128, NB * QP], "bfloat16"),
     "pp": ("sbuf", [128, NB * PW], "bfloat16"),
     "ysb": ("sbuf", [128, QP], "bfloat16"),
-    "pS0": ("psum", [128, 512], "float32"),
-    "pS1": ("psum", [128, 512], "float32"),
-    "pT0": ("psum", [128, 512], "float32"),
-    "pT1": ("psum", [128, 512], "float32"),
-    "pT2": ("psum", [128, 512], "float32"),
-    "pT3": ("psum", [128, 512], "float32"),
+    "pA0": ("psum", [128, 512], "float32"),
+    "pA1": ("psum", [128, 512], "float32"),
+    "pA2": ("psum", [128, 512], "float32"),
+    "pB0": ("psum", [128, 512], "float32"),
+    "pB1": ("psum", [128, 512], "float32"),
+    "pB2": ("psum", [128, 512], "float32"),
     "pH": ("psum", [128, 512], "float32"),
     "pY": ("psum", [128, 512], "float32"),
 }
 SEMAPHORES = (["a%d" % i for i in range(NB)] + ["b%d" % i for i in range(NB)] + ["c%d" % i for i in range(NB)] +
               ["f%d" % i for i in range(len(BATCHES))] +
-              ["hv", "ldk", "ldv", "ldq", "vi", "di", "di2", "vc", "st", "ss", "vacc", "vm", "sm", "vr", "vd", "sh",
-               "vh", "sp", "sy", "vq", "vy", "sto", "sent"])
+              ["hv", "ldk", "ldv", "ldq", "vi", "di", "di2", "vc", "st", "ss", "sa", "vacc", "vpre", "vr", "vd", "sh",
+               "sh2", "vh", "sp", "sy", "vq", "vy", "sto", "sent"])
 
 
 def _bits(m):
@@ -179,10 +179,10 @@ def rank_program(g, core, T, topo):
     ve.memset(T.ida[:, 0:1], 1.0).then_inc(sem.vi, 1)
     ve.memset(T.half[:], 0.5).then_inc(sem.vc, 1)
     ve.memset(T.pp[:], 1.0).then_inc(sem.vc, 1)
-    sc.wait_ge(sem.vi, 2)
-    sc.dma_start(T.idd[:], T.ida[:]).then_inc(sem.di, 16)
-    sc.wait_ge(sem.di, 16)
-    sc.dma_start(T.ident[:], T.idd[0:128, :]).then_inc(sem.di2, 16)
+    sy.wait_ge(sem.vi, 2)
+    sy.dma_start(T.idd[:], T.ida[:]).then_inc(sem.di, 16)
+    sy.wait_ge(sem.di, 16)
+    sy.dma_start(T.ident[:], T.idd[0:128, :]).then_inc(sem.di2, 16)
 
     sent = 0
     g.wait_ge(sem.ldk, 16)
@@ -223,14 +223,12 @@ def rank_program(g, core, T, topo):
             est[nch + s] = (t, b)
     order = [(s, est[s][1]) for s in sorted(est, key=lambda x: (est[x][0], x))]
 
-    pT = [T.pT0, T.pT1, T.pT2, T.pT3]
-    pS = [T.pS0, T.pS1]
-
-    def sblk(i):
-        return pS[i // 8][:, (i % 8) * QP:(i % 8 + 1) * QP]
+    pA = [T.pA0, T.pA1, T.pA2]
+    pB = [T.pB0, T.pB1, T.pB2]
 
     units = [[i, i + 1] for i in range(0, NB - SOLO, 2)] + [[i] for i in range(NB - SOLO, NB)]
-    npair = (NB - SOLO) // 2
+    NU = len(units)
+    last = pA[(NU - 1) % NT]
 
     te.wait_ge(sem.ldq, 16)
     for u, unit in enumerate(units):
@@ -244,16 +242,20 @@ def rank_program(g, core, T, topo):
                 te.wait_ge(sem["f%d" % b], fcount[b])
             if j == 0 and u >= NT:
                 te.wait_ge(sem.vacc, u - NT + 1)
-            mm = te.matmul(pT[u % NT][:, j * QP:(j + 1) * QP], kblk(s), q, True, True)
+                te.wait_ge(sem.sa, u - NT + 1)
+            if u == NU - 1:
+                te.wait_ge(sem.vpre, 1)
+            mm = te.matmul(pA[u % NT][0:QP, j * W:(j + 1) * W], q, kblk(s), True, True)
             if j == len(unit) - 1:
                 mm.then_inc(sem.st, 1)
-            te.matmul(sblk(i), kblk(s), q, True, True).then_inc(sem.ss, 1)
-    te.wait_ge(sem.di2, 16)
-    te.wait_ge(sem.vm, 1)
-    te.matmul(T.pT0[0:QP, 0:128], T.accb[:], T.ident[:], True, True).then_inc(sem.sm, 1)
+            mm = te.matmul(pB[u % NT][:, j * QP:(j + 1) * QP], kblk(s), q, True, True)
+            if j == len(unit) - 1:
+                mm.then_inc(sem.ss, 1)
     te.wait_ge(sem.vc, NC)
     te.wait_ge(sem.vd, 1)
     te.matmul(T.pH[:, 0:QP], T.half[0:QP, :], T.diag[0:QP, :], True, True).then_inc(sem.sh, 1)
+    te.wait_ge(sem.sa, NU)
+    te.matmul(T.pB0[:, 0:QP], T.half[0:QP, :], T.diag[0:QP, :], True, True).then_inc(sem.sh2, 1)
     hs = helpers(ci, od)
     for i, (s, b) in enumerate(order):
         r = slot_rank(s)
@@ -268,39 +270,32 @@ def rank_program(g, core, T, topo):
         if i == NB - 1:
             mm.then_inc(sem.sy, 1)
 
-    acc = T.acc
-    nv = 0
     for u, unit in enumerate(units):
+        sc.wait_ge(sem.ss, u + 1)
+        sc.activation(T.ssb[:, unit[0] * QP:(unit[-1] + 1) * QP], pB[u % NT][:, 0:len(unit) * QP],
+                      ActivationFunctionType.Copy).then_inc(sem.sa, 1)
+    sc.wait_ge(sem.sh2, 1)
+    sc.activation(T.hb[:], T.pB0[:, 0:QP], ActivationFunctionType.Copy).then_inc(sem.vh, 1)
+
+    for u, unit in enumerate(units[:-1]):
         ve.wait_ge(sem.st, u + 1)
-        bank = pT[u % NT]
-        if nv:
-            ve.wait_ge(sem.vacc, nv)
-        if u == 0:
-            ve.tensor_copy(acc[:], bank[:, 0:2 * QP]).then_inc(sem.vacc, 1)
-        elif u < npair:
-            ve.tensor_tensor(acc[:], bank[:, 0:2 * QP], acc[:], AluOpType.max).then_inc(sem.vacc, 1)
-        elif u < len(units) - 1:
-            ve.tensor_tensor(acc[:, 0:QP], bank[:, 0:QP], acc[:, 0:QP], AluOpType.max).then_inc(sem.vacc, 1)
-        else:
-            ve.tensor_tensor(T.accb[:], bank[:, 0:QP], acc[:, 0:QP], AluOpType.max).then_inc(sem.vm, 1)
-            break
-        nv += 1
-        if u == npair - 1:
-            ve.wait_ge(sem.vacc, nv)
-            ve.tensor_tensor(acc[:, 0:QP], acc[:, 0:QP], acc[:, QP:2 * QP], AluOpType.max).then_inc(sem.vacc, 1)
-            nv += 1
-    ve.wait_ge(sem.sm, 1)
-    ve.tensor_reduce(T.mcol[0:QP, 0:1], T.pT0[0:QP, 0:128], AxisListType.X, AluOpType.max).then_inc(sem.vr, 1)
+        ve.tensor_reduce(T.mcols[0:QP, u:u + 1], pA[u % NT][0:QP, 0:len(unit) * W], AxisListType.X,
+                         AluOpType.max).then_inc(sem.vacc, 1)
+    ve.wait_ge(sem.vacc, NU - 1)
+    ve.tensor_reduce(last[0:QP, W:W + 1], T.mcols[0:QP, 0:NU - 1], AxisListType.X, AluOpType.max).then_inc(sem.vpre, 1)
+    ve.wait_ge(sem.vpre, 1)
+    ve.wait_ge(sem.st, NU)
+    ve.tensor_reduce(T.mfin[0:QP, 0:1], last[0:QP, 0:W + 1], AxisListType.X, AluOpType.max).then_inc(sem.vr, 1)
     ve.wait_ge(sem.vr, 1)
     ve.wait_ge(sem.di2, 16)
-    ve.tensor_scalar(T.diag[0:QP, :], T.ident[0:QP, 0:QP], T.mcol[0:QP, 0:1], None, AluOpType.mult).then_inc(sem.vd, 1)
-    ve.wait_ge(sem.sh, 1)
-    ve.tensor_copy(T.hb[:], T.pH[:, 0:QP]).then_inc(sem.vh, 1)
-    ve.wait_ge(sem.vh, 1)
+    ve.tensor_scalar(T.diag[0:QP, :], T.ident[0:QP, 0:QP], T.mfin[0:QP, 0:1], None, AluOpType.mult).then_inc(sem.vd, 1)
     ve.wait_ge(sem.vc, NC)
-    ve.wait_ge(sem.ss, NB)
+    ve.wait_ge(sem.sa, NU)
+    ve.wait_ge(sem.sh, 1)
     for i in range(NB):
-        ve.tensor_tensor(T.pp[:, i * PW:i * PW + QP], sblk(i), T.hb[:], AluOpType.max).then_inc(sem.sp, 1)
+        ve.tensor_tensor(T.pp[:, i * PW:i * PW + QP], T.ssb[:, i * QP:(i + 1) * QP], T.pH[:, 0:QP],
+                         AluOpType.max).then_inc(sem.sp, 1)
+    ve.wait_ge(sem.vh, 1)
     ve.wait_ge(sem.sy, 1)
     ve.tensor_scalar(T.cc[:], T.hb[:], T.pY[:, QP:QP + 1], None, AluOpType.mult).then_inc(sem.vq, 1)
     ve.wait_ge(sem.vq, 1)

@@ -10,15 +10,15 @@ WAVES = [[1, 2], [3, 4], [5, 6], [7]]
 BATCHES = [[0], [1, 2], [3, 4], [5, 6], [7]]
 NT = 3
 SOLO = 2
+NVIA = 2
 HOP = 24
 
 SCRATCH = {
     "kk": ("sbuf", [128, NB * W], "bfloat16"),
     "vv": ("sbuf", [128, NB * W], "bfloat16"),
     "qq": ("sbuf", [128, QP], "bfloat16"),
-    "ida": ("sbuf", [128, 129], "bfloat16"),
-    "idd": ("dram", [129, 128], "bfloat16"),
-    "ident": ("sbuf", [128, 128], "bfloat16"),
+    "onesq": ("sbuf", [128, QP], "bfloat16"),
+    "ident": ("sbuf", [128, QP], "bfloat16"),
     "half": ("sbuf", [128, 128], "bfloat16"),
     "mcols": ("sbuf", [128, 16], "float32"),
     "mfin": ("sbuf", [128, 8], "float32"),
@@ -39,8 +39,8 @@ SCRATCH = {
 }
 SEMAPHORES = (["a%d" % i for i in range(NB)] + ["b%d" % i for i in range(NB)] + ["c%d" % i for i in range(NB)] +
               ["f%d" % i for i in range(len(BATCHES))] +
-              ["hv", "ldk", "ldv", "ldq", "vi", "di", "di2", "vc", "st", "ss", "sa", "vacc", "vpre", "vr", "vd", "sh",
-               "sh2", "vh", "sp", "sy", "vq", "vy", "sto", "sent"])
+              ["hv", "ldk", "ldv", "ldq", "vi", "vo", "gi", "cx", "vc", "st", "ss", "sa", "vacc", "vpre", "vr", "vd",
+               "sh", "sh2", "vh", "sp", "sy", "vq", "vy", "sto", "sent"])
 
 
 def _bits(m):
@@ -58,13 +58,19 @@ def rank_program(g, core, T, topo):
     te, ve, sy, sc = g.tensor, g.vector, g.sync, g.scalar
 
     chips = sorted(set(topo.chip(c) for c in T.cores))
-    if topo.chip(core) not in chips:
-        return
     nch = len(chips)
-    ci = chips.index(topo.chip(core))
-    d = topo.die(core)
-    od = [topo.die(c) for c in T.cores if topo.chip(c) == topo.chip(core) and topo.die(c) != d][0]
     everyone = range(topo.CHIPS * topo.CORES_PER_CHIP)
+
+    def mate_of(ch):
+        return [x for x in range(topo.CHIPS) if topo.mates(ch, x)][0]
+
+    guest = topo.chip(core) not in chips
+    home = mate_of(topo.chip(core)) if guest else topo.chip(core)
+    if home not in chips:
+        return
+    ci = chips.index(home)
+    d = topo.die(core)
+    od = [topo.die(c) for c in T.cores if topo.chip(c) == home and topo.die(c) != d][0]
 
     def rank_at(i, dd):
         return [c for c in T.cores if topo.chip(c) == chips[i] and topo.die(c) == dd][0]
@@ -74,8 +80,34 @@ def rank_program(g, core, T, topo):
         cand.sort(key=lambda h: (-sum(1 for c in T.cores if topo.may_write(h, c)), h))
         return cand[:2]
 
+    def port_chip(a, b):
+        if topo.same_plane(a, b):
+            return a
+        if topo.mates(a, b):
+            return None
+        return mate_of(a)
+
+    outload = {}
+    for a in chips:
+        for b in chips:
+            if a != b and port_chip(a, b) is not None:
+                outload[port_chip(a, b)] = outload.get(port_chip(a, b), 0) + 1
+    via = {}
+    for b in chips:
+        cand = [] if mate_of(b) in chips else [a for a in chips if a != b and port_chip(a, b) not in (a, None)]
+        cand.sort(key=lambda a: (outload.get(a, 0) - outload.get(mate_of(a), 0), a))
+        via[b] = cand[:NVIA]
+
+    def detour(i, s):
+        return chips[i] in via[chips[(i + s) % nch]]
+
     def recv(i, s, dd):
-        return helpers((i + s) % nch, dd)[s % 2]
+        j = (i + s) % nch
+        if detour(i, s):
+            cand = [c for c in everyone if topo.chip(c) == mate_of(chips[j]) and topo.die(c) == dd and
+                    topo.may_write(c, rank_at(j, dd))]
+            return cand[via[chips[j]].index(chips[i])]
+        return helpers(j, dd)[s % 2]
 
     def vplan(i, dd):
         hl = helpers(i, dd)
@@ -86,7 +118,7 @@ def rank_program(g, core, T, topo):
             load[h].append(s)
         plan = {}
         for h in hl:
-            steps = sorted(load[h])
+            steps = sorted(load[h], key=lambda x: (not detour(i, x), x))
             for w in range(0, len(steps), 2):
                 wave = steps[w:w + 2]
                 ms = _split(topo.mask(h, recv(i, wave[0], dd)), len(wave))
@@ -111,34 +143,38 @@ def rank_program(g, core, T, topo):
         return (m_on & ~topo.mask(a, off_chip)) or m_on
 
     if T.rank_of(core) is None:
-        hl = helpers(ci, d)
-        if core not in hl:
-            return
         mine, other = rank_at(ci, d), rank_at(ci, od)
-        r0 = T.rank_of(mine)
-        sent = 0
-        g.wait_ge(sem.hv, _bits(_split(stay(mine, core, rank_at((ci + 1) % nch, d)), 2)[0]))
-        waves = {}
-        for s, (h, w, m) in vplan(ci, d).items():
-            if h == core:
-                waves.setdefault(w, []).append((s, m))
-        for w in sorted(waves):
-            trs = []
-            for s, m in sorted(waves[w]):
-                trs.append(transfer(recv(ci, s, d), m, sem["c%d" % r0], vblk(r0), vblk(r0)))
-                sent += _bits(m)
-            g.remote_dma_fused(trs, local_sem=sem.sent)
-        if hl.index(core) == 1:
-            m = stay(core, other, recv(ci, 1, d))
-            rid, pid, _ = topo.addr(other)
-            g.remote_dma(vblk(r0), vblk(r0), sem["b%d" % r0], sem.sent, pid, rid, m)
-            sent += _bits(m)
         inc = []
         for s in range(1, nch):
             cs = (ci - s) % nch
             if recv(cs, s, d) == core:
                 h, w, m = vplan(cs, d)[s]
                 inc.append((w, s, T.rank_of(rank_at(cs, d)), _bits(m)))
+        sent = 0
+        if guest:
+            if not inc:
+                return
+        else:
+            hl = helpers(ci, d)
+            if core not in hl:
+                return
+            r0 = T.rank_of(mine)
+            g.wait_ge(sem.hv, _bits(_split(stay(mine, core, rank_at((ci + 1) % nch, d)), 2)[0]))
+            waves = {}
+            for s, (h, w, m) in vplan(ci, d).items():
+                if h == core:
+                    waves.setdefault(w, []).append((s, m))
+            for w in sorted(waves):
+                trs = []
+                for s, m in sorted(waves[w]):
+                    trs.append(transfer(recv(ci, s, d), m, sem["c%d" % r0], vblk(r0), vblk(r0)))
+                    sent += _bits(m)
+                g.remote_dma_fused(trs, local_sem=sem.sent)
+            if hl.index(core) == 1:
+                m = stay(core, other, recv(ci, 1, d))
+                rid, pid, _ = topo.addr(other)
+                g.remote_dma(vblk(r0), vblk(r0), sem["b%d" % r0], sem.sent, pid, rid, m)
+                sent += _bits(m)
         lo, hi = _split(topo.mask(core, other), 2)
         for w, s, r, n in sorted(inc):
             g.wait_ge(sem["c%d" % r], n)
@@ -174,17 +210,17 @@ def rank_program(g, core, T, topo):
     sc.dma_start(vblk(me), T.v[:]).then_inc(sem.ldv, 16)
     sy.dma_start(q, T.q[:]).then_inc(sem.ldq, 16)
 
-    NC = 2
-    ve.memset(T.ida[:, 1:129], 0.0).then_inc(sem.vi, 1)
-    ve.memset(T.ida[:, 0:1], 1.0).then_inc(sem.vi, 1)
-    ve.memset(T.half[:], 0.5).then_inc(sem.vc, 1)
-    ve.memset(T.pp[:], 1.0).then_inc(sem.vc, 1)
-    sy.wait_ge(sem.vi, 2)
-    sy.dma_start(T.idd[:], T.ida[:]).then_inc(sem.di, 16)
-    sy.wait_ge(sem.di, 16)
-    sy.dma_start(T.ident[:], T.idd[0:128, :]).then_inc(sem.di2, 16)
-
+    srid, spid, _ = topo.addr(sib)
     sent = 0
+    first = me < T.rank_of(sib)
+    hpart = T.half[:, 0:QP] if first else T.half[:, QP:2 * QP]
+    ve.memset(hpart, 0.5).then_inc(sem.vi, 1)
+    g.wait_ge(sem.vi, 1)
+    g.remote_dma(hpart, hpart, sem.cx, sem.sent, spid, srid, m_off)
+    sent += _bits(m_off)
+    ve.memset(T.onesq[:], 1.0).then_inc(sem.vo, 1)
+    ve.memset(T.pp[:], 1.0).then_inc(sem.vc, 1)
+
     g.wait_ge(sem.ldk, 16)
     for wave in WAVES:
         trs = []
@@ -198,7 +234,6 @@ def rank_program(g, core, T, topo):
         trs.append(transfer(h, m, sem.hv, vblk(me), vblk(me)))
         sent += _bits(m)
     g.remote_dma_fused(trs, local_sem=sem.sent)
-    srid, spid, _ = topo.addr(sib)
     fcount = []
     for b, batch in enumerate(BATCHES):
         for s in batch:
@@ -209,6 +244,9 @@ def rank_program(g, core, T, topo):
                      spid, srid, m)
         sent += _bits(m)
         fcount.append(_bits(m))
+        if b == 0:
+            g.wait_ge(sem.vo, 1)
+            g.affine_select(T.ident[:], T.onesq[:], [[-1, QP]], AluOpType.is_equal, 0.0, 0, 1).then_inc(sem.gi, 1)
     g.wait_ge(sem.sent, sent)
 
     est = {0: (0, None)}
@@ -251,12 +289,14 @@ def rank_program(g, core, T, topo):
             mm = te.matmul(pB[u % NT][:, j * QP:(j + 1) * QP], kblk(s), q, True, True)
             if j == len(unit) - 1:
                 mm.then_inc(sem.ss, 1)
-    te.wait_ge(sem.vc, NC)
+    te.wait_ge(sem.vi, 1)
+    te.wait_ge(sem.cx, _bits(m_off))
     te.wait_ge(sem.vd, 1)
     te.matmul(T.pH[:, 0:QP], T.half[0:QP, :], T.diag[0:QP, :], True, True).then_inc(sem.sh, 1)
     te.wait_ge(sem.sa, NU)
     te.matmul(T.pB0[:, 0:QP], T.half[0:QP, :], T.diag[0:QP, :], True, True).then_inc(sem.sh2, 1)
     hs = helpers(ci, od)
+    te.wait_ge(sem.vc, 1)
     for i, (s, b) in enumerate(order):
         r = slot_rank(s)
         if r == me:
@@ -264,7 +304,8 @@ def rank_program(g, core, T, topo):
         elif s == nch:
             te.wait_ge(sem["b%d" % r], _bits(stay(hs[1], core, recv(ci, 1, od))))
         else:
-            te.wait_ge(sem["b%d" % r], _bits(_split(topo.mask(hs[0], core), 2)[0]))
+            rc = recv((ci - s) % nch, s % nch, d if s < nch else od)
+            te.wait_ge(sem["b%d" % r], _bits(_split(topo.mask(rc, core), 2)[0]))
         te.wait_ge(sem.sp, i + 1)
         mm = te.matmul(T.pY[:, 0:PN], vblk(r), T.pp[:, i * PW:i * PW + PN], i == 0, i == NB - 1)
         if i == NB - 1:
@@ -287,9 +328,9 @@ def rank_program(g, core, T, topo):
     ve.wait_ge(sem.st, NU)
     ve.tensor_reduce(T.mfin[0:QP, 0:1], last[0:QP, 0:W + 1], AxisListType.X, AluOpType.max).then_inc(sem.vr, 1)
     ve.wait_ge(sem.vr, 1)
-    ve.wait_ge(sem.di2, 16)
+    ve.wait_ge(sem.gi, 1)
     ve.tensor_scalar(T.diag[0:QP, :], T.ident[0:QP, 0:QP], T.mfin[0:QP, 0:1], None, AluOpType.mult).then_inc(sem.vd, 1)
-    ve.wait_ge(sem.vc, NC)
+    ve.wait_ge(sem.vc, 1)
     ve.wait_ge(sem.sa, NU)
     ve.wait_ge(sem.sh, 1)
     for i in range(NB):

from concourse.bass import DstId, RemoteDMATransfer
from concourse.mybir import AluOpType, AxisListType, ActivationFunctionType

NB = 16
W = 128
QP = 64
PW = 72
PN = 66
WAVES = [[1, 2], [3, 4], [5, 6], [7]]
BATCHES = [[0], [1, 2], [3, 4], [5, 6], [7]]
NT = 3
SOLO = 2
NVIA = 2
HOP = 24

SCRATCH = {
    "kk": ("sbuf", [128, NB * W], "bfloat16"),
    "vv": ("sbuf", [128, NB * W], "bfloat16"),
    "qq": ("sbuf", [128, QP], "bfloat16"),
    "onesq": ("sbuf", [128, QP], "bfloat16"),
    "ident": ("sbuf", [128, QP], "bfloat16"),
    "half": ("sbuf", [128, 128], "bfloat16"),
    "mcols": ("sbuf", [128, 16], "float32"),
    "mfin": ("sbuf", [128, 8], "float32"),
    "diag": ("sbuf", [128, QP], "bfloat16"),
    "hb": ("sbuf", [128, QP], "bfloat16"),
    "cc": ("sbuf", [128, QP], "float32"),
    "ssb": ("sbuf", [128, NB * QP], "bfloat16"),
    "pp": ("sbuf", [128, NB * PW], "bfloat16"),
    "ysb": ("sbuf", [128, QP], "bfloat16"),
    "pA0": ("psum", [128, 512], "float32"),
    "pA1": ("psum", [128, 512], "float32"),
    "pA2": ("psum", [128, 512], "float32"),
    "pB0": ("psum", [128, 512], "float32"),
    "pB1": ("psum", [128, 512], "float32"),
    "pB2": ("psum", [128, 512], "float32"),
    "pH": ("psum", [128, 512], "float32"),
    "pY": ("psum", [128, 512], "float32"),
}
SEMAPHORES = (["a%d" % i for i in range(NB)] + ["b%d" % i for i in range(NB)] + ["c%d" % i for i in range(NB)] +
              ["f%d" % i for i in range(len(BATCHES))] +
              ["hv", "ldk", "ldv", "ldq", "vi", "vo", "gi", "cx", "vc", "st", "ss", "sa", "vacc", "vpre", "vr", "vd",
               "sh", "sh2", "vh", "sp", "sy", "vq", "vy", "sto", "sent"])


def _bits(m):
    return bin(m).count("1")


def _split(mask, n):
    eng = [e for e in range(32) if (mask >> e) & 1]
    per = len(eng) // n
    return [sum(1 << e for e in eng[j * per:(j + 1) * per]) for j in range(n)]


def rank_program(g, core, T, topo):
    sem = T.sem
    te, ve, sy, sc = g.tensor, g.vector, g.sync, g.scalar

    chips = sorted(set(topo.chip(c) for c in T.cores))
    nch = len(chips)
    everyone = range(topo.CHIPS * topo.CORES_PER_CHIP)

    def mate_of(ch):
        return [x for x in range(topo.CHIPS) if topo.mates(ch, x)][0]

    guest = topo.chip(core) not in chips
    home = mate_of(topo.chip(core)) if guest else topo.chip(core)
    if home not in chips:
        return
    ci = chips.index(home)
    d = topo.die(core)
    od = [topo.die(c) for c in T.cores if topo.chip(c) == home and topo.die(c) != d][0]

    def rank_at(i, dd):
        return [c for c in T.cores if topo.chip(c) == chips[i] and topo.die(c) == dd][0]

    def helpers(i, dd):
        cand = [c for c in everyone if topo.chip(c) == chips[i] and topo.die(c) == dd and T.rank_of(c) is None]
        cand.sort(key=lambda h: (-sum(1 for c in T.cores if topo.may_write(h, c)), h))
        return cand[:2]

    def port_chip(a, b):
        if topo.same_plane(a, b):
            return a
        if topo.mates(a, b):
            return None
        return mate_of(a)

    outload = {}
    for a in chips:
        for b in chips:
            if a != b and port_chip(a, b) is not None:
                outload[port_chip(a, b)] = outload.get(port_chip(a, b), 0) + 1
    via = {}
    for b in chips:
        cand = [] if mate_of(b) in chips else [a for a in chips if a != b and port_chip(a, b) not in (a, None)]
        cand.sort(key=lambda a: (outload.get(a, 0) - outload.get(mate_of(a), 0), a))
        via[b] = cand[:NVIA]

    def detour(i, s):
        return chips[i] in via[chips[(i + s) % nch]]

    def recv(i, s, dd):
        j = (i + s) % nch
        if detour(i, s):
            cand = [c for c in everyone if topo.chip(c) == mate_of(chips[j]) and topo.die(c) == dd and
                    topo.may_write(c, rank_at(j, dd))]
            return cand[via[chips[j]].index(chips[i])]
        return helpers(j, dd)[s % 2]

    def vplan(i, dd):
        hl = helpers(i, dd)
        load = dict((h, []) for h in hl)
        can = dict((s, [h for h in hl if topo.may_write(h, recv(i, s, dd))]) for s in range(1, nch))
        for s in sorted(can, key=lambda x: (len(can[x]), x)):
            h = min(can[s], key=lambda x: (len(load[x]), -hl.index(x)))
            load[h].append(s)
        plan = {}
        for h in hl:
            steps = sorted(load[h], key=lambda x: (not detour(i, x), x))
            for w in range(0, len(steps), 2):
                wave = steps[w:w + 2]
                ms = _split(topo.mask(h, recv(i, wave[0], dd)), len(wave))
                for j, s in enumerate(wave):
                    plan[s] = (h, w // 2, ms[j])
        return plan

    def kblk(lo, hi=None):
        hi = lo if hi is None else hi
        return T.kk[:, lo * W:(hi + 1) * W]

    def vblk(r):
        return T.vv[:, r * W:(r + 1) * W]

    def transfer(dst, mask, rsem, src_ap, dst_ap):
        rid, pid, _ = topo.addr(dst)
        return RemoteDMATransfer(dst_ids=[DstId(rid=rid, pnc=pid)], dma_engine_mask=mask, remote_sem=rsem,
                                 srcs=[src_ap], dsts=[dst_ap], alu_op=0)

    def stay(a, on_chip, off_chip):
        m_on = topo.mask(a, on_chip)
        return (m_on & ~topo.mask(a, off_chip)) or m_on

    if T.rank_of(core) is None:
        mine, other = rank_at(ci, d), rank_at(ci, od)
        inc = []
        for s in range(1, nch):
            cs = (ci - s) % nch
            if recv(cs, s, d) == core:
                h, w, m = vplan(cs, d)[s]
                inc.append((w, s, T.rank_of(rank_at(cs, d)), _bits(m)))
        sent = 0
        if guest:
            if not inc:
                return
        else:
            hl = helpers(ci, d)
            if core not in hl:
                return
            r0 = T.rank_of(mine)
            g.wait_ge(sem.hv, _bits(_split(stay(mine, core, rank_at((ci + 1) % nch, d)), 2)[0]))
            waves = {}
            for s, (h, w, m) in vplan(ci, d).items():
                if h == core:
                    waves.setdefault(w, []).append((s, m))
            for w in sorted(waves):
                trs = []
                for s, m in sorted(waves[w]):
                    trs.append(transfer(recv(ci, s, d), m, sem["c%d" % r0], vblk(r0), vblk(r0)))
                    sent += _bits(m)
                g.remote_dma_fused(trs, local_sem=sem.sent)
            if hl.index(core) == 1:
                m = stay(core, other, recv(ci, 1, d))
                rid, pid, _ = topo.addr(other)
                g.remote_dma(vblk(r0), vblk(r0), sem["b%d" % r0], sem.sent, pid, rid, m)
                sent += _bits(m)
        lo, hi = _split(topo.mask(core, other), 2)
        for w, s, r, n in sorted(inc):
            g.wait_ge(sem["c%d" % r], n)
            g.remote_dma_fused([transfer(mine, lo, sem["b%d" % r], vblk(r), vblk(r)),
                                transfer(other, hi, sem["b%d" % r], vblk(r), vblk(r))], local_sem=sem.sent)
            sent += _bits(lo) + _bits(hi)
        g.wait_ge(sem.sent, sent)
        return

    me = T.rank_of(core)
    sib = rank_at(ci, od)
    dest = {}
    for s in range(1, nch):
        dest[s] = rank_at((ci + s) % nch, d)
        assert topo.may_write(core, dest[s])
    m_off = topo.mask(core, dest[1])
    m_on = topo.mask(core, sib)
    m_stay = stay(core, sib, dest[1])
    smask = {}
    for wave in WAVES:
        for s, m in zip(wave, _split(m_off, len(wave))):
            smask[s] = m

    def asem(s):
        return sem["a%d" % T.rank_of(rank_at((ci - s) % nch, d))]

    def slot_rank(s):
        return T.rank_of(rank_at((ci - s) % nch, d)) if s < nch else T.rank_of(rank_at((ci - s) % nch, od))

    q = T.qq[:]

    sy.dma_start(kblk(0), T.k[:]).then_inc(sem.ldk, 16)
    sc.dma_start(vblk(me), T.v[:]).then_inc(sem.ldv, 16)
    sy.dma_start(q, T.q[:]).then_inc(sem.ldq, 16)

    srid, spid, _ = topo.addr(sib)
    sent = 0
    first = me < T.rank_of(sib)
    hpart = T.half[:, 0:QP] if first else T.half[:, QP:2 * QP]
    ve.memset(hpart, 0.5).then_inc(sem.vi, 1)
    g.wait_ge(sem.vi, 1)
    g.remote_dma(hpart, hpart, sem.cx, sem.sent, spid, srid, m_off)
    sent += _bits(m_off)
    ve.memset(T.onesq[:], 1.0).then_inc(sem.vo, 1)
    ve.memset(T.pp[:], 1.0).then_inc(sem.vc, 1)

    g.wait_ge(sem.ldk, 16)
    for wave in WAVES:
        trs = []
        for s in wave:
            trs.append(transfer(dest[s], smask[s], sem["a%d" % me], kblk(0), kblk(s)))
            sent += _bits(smask[s])
        g.remote_dma_fused(trs, local_sem=sem.sent)
    g.wait_ge(sem.ldv, 16)
    trs = []
    for h, m in zip(helpers(ci, d), _split(m_stay, 2)):
        trs.append(transfer(h, m, sem.hv, vblk(me), vblk(me)))
        sent += _bits(m)
    g.remote_dma_fused(trs, local_sem=sem.sent)
    fcount = []
    for b, batch in enumerate(BATCHES):
        for s in batch:
            if s > 0:
                g.wait_ge(asem(s), _bits(smask[s]))
        m = m_on if b == len(BATCHES) - 1 else m_stay
        g.remote_dma(kblk(nch + batch[0], nch + batch[-1]), kblk(batch[0], batch[-1]), sem["f%d" % b], sem.sent,
                     spid, srid, m)
        sent += _bits(m)
        fcount.append(_bits(m))
        if b == 0:
            g.wait_ge(sem.vo, 1)
            g.affine_select(T.ident[:], T.onesq[:], [[-1, QP]], AluOpType.is_equal, 0.0, 0, 1).then_inc(sem.gi, 1)
    g.wait_ge(sem.sent, sent)

    est = {0: (0, None)}
    t = 0
    for wave in WAVES:
        t += 16 * len(wave)
        for s in wave:
            est[s] = (t, None)
    for b, batch in enumerate(BATCHES):
        t = max(est[s][0] for s in batch) + HOP + 16 * len(batch) - (40 if b == 0 else 0)
        for s in batch:
            est[nch + s] = (t, b)
    order = [(s, est[s][1]) for s in sorted(est, key=lambda x: (est[x][0], x))]

    pA = [T.pA0, T.pA1, T.pA2]
    pB = [T.pB0, T.pB1, T.pB2]

    units = [[i, i + 1] for i in range(0, NB - SOLO, 2)] + [[i] for i in range(NB - SOLO, NB)]
    NU = len(units)
    last = pA[(NU - 1) % NT]

    te.wait_ge(sem.ldq, 16)
    for u, unit in enumerate(units):
        for j, i in enumerate(unit):
            s, b = order[i]
            if s == 0:
                te.wait_ge(sem.ldk, 16)
            elif b is None:
                te.wait_ge(asem(s), _bits(smask[s]))
            else:
                te.wait_ge(sem["f%d" % b], fcount[b])
            if j == 0 and u >= NT:
                te.wait_ge(sem.vacc, u - NT + 1)
                te.wait_ge(sem.sa, u - NT + 1)
            if u == NU - 1:
                te.wait_ge(sem.vpre, 1)
            mm = te.matmul(pA[u % NT][0:QP, j * W:(j + 1) * W], q, kblk(s), True, True)
            if j == len(unit) - 1:
                mm.then_inc(sem.st, 1)
            mm = te.matmul(pB[u % NT][:, j * QP:(j + 1) * QP], kblk(s), q, True, True)
            if j == len(unit) - 1:
                mm.then_inc(sem.ss, 1)
    te.wait_ge(sem.vi, 1)
    te.wait_ge(sem.cx, _bits(m_off))
    te.wait_ge(sem.vd, 1)
    te.matmul(T.pH[:, 0:QP], T.half[0:QP, :], T.diag[0:QP, :], True, True).then_inc(sem.sh, 1)
    te.wait_ge(sem.sa, NU)
    te.matmul(T.pB0[:, 0:QP], T.half[0:QP, :], T.diag[0:QP, :], True, True).then_inc(sem.sh2, 1)
    hs = helpers(ci, od)
    te.wait_ge(sem.vc, 1)
    for i, (s, b) in enumerate(order):
        r = slot_rank(s)
        if r == me:
            te.wait_ge(sem.ldv, 16)
        elif s == nch:
            te.wait_ge(sem["b%d" % r], _bits(stay(hs[1], core, recv(ci, 1, od))))
        else:
            rc = recv((ci - s) % nch, s % nch, d if s < nch else od)
            te.wait_ge(sem["b%d" % r], _bits(_split(topo.mask(rc, core), 2)[0]))
        te.wait_ge(sem.sp, i + 1)
        mm = te.matmul(T.pY[:, 0:PN], vblk(r), T.pp[:, i * PW:i * PW + PN], i == 0, i == NB - 1)
        if i == NB - 1:
            mm.then_inc(sem.sy, 1)

    for u, unit in enumerate(units):
        sc.wait_ge(sem.ss, u + 1)
        sc.activation(T.ssb[:, unit[0] * QP:(unit[-1] + 1) * QP], pB[u % NT][:, 0:len(unit) * QP],
                      ActivationFunctionType.Copy).then_inc(sem.sa, 1)
    sc.wait_ge(sem.sh2, 1)
    sc.activation(T.hb[:], T.pB0[:, 0:QP], ActivationFunctionType.Copy).then_inc(sem.vh, 1)

    for u, unit in enumerate(units[:-1]):
        ve.wait_ge(sem.st, u + 1)
        ve.tensor_reduce(T.mcols[0:QP, u:u + 1], pA[u % NT][0:QP, 0:len(unit) * W], AxisListType.X,
                         AluOpType.max).then_inc(sem.vacc, 1)
    ve.wait_ge(sem.vacc, NU - 1)
    ve.tensor_reduce(last[0:QP, W:W + 1], T.mcols[0:QP, 0:NU - 1], AxisListType.X, AluOpType.max).then_inc(sem.vpre, 1)
    ve.wait_ge(sem.vpre, 1)
    ve.wait_ge(sem.st, NU)
    ve.tensor_reduce(T.mfin[0:QP, 0:1], last[0:QP, 0:W + 1], AxisListType.X, AluOpType.max).then_inc(sem.vr, 1)
    ve.wait_ge(sem.vr, 1)
    ve.wait_ge(sem.gi, 1)
    ve.tensor_scalar(T.diag[0:QP, :], T.ident[0:QP, 0:QP], T.mfin[0:QP, 0:1], None, AluOpType.mult).then_inc(sem.vd, 1)
    ve.wait_ge(sem.vc, 1)
    ve.wait_ge(sem.sa, NU)
    ve.wait_ge(sem.sh, 1)
    for i in range(NB):
        ve.tensor_tensor(T.pp[:, i * PW:i * PW + QP], T.ssb[:, i * QP:(i + 1) * QP], T.pH[:, 0:QP],
                         AluOpType.max).then_inc(sem.sp, 1)
    ve.wait_ge(sem.vh, 1)
    ve.wait_ge(sem.sy, 1)
    ve.tensor_scalar(T.cc[:], T.hb[:], T.pY[:, QP:QP + 1], None, AluOpType.mult).then_inc(sem.vq, 1)
    ve.wait_ge(sem.vq, 1)
    ve.tensor_tensor(T.ysb[:], T.pY[:, 0:QP], T.cc[:], AluOpType.subtract).then_inc(sem.vy, 1)

    sy.wait_ge(sem.vy, 1)
    sy.dma_start(T.y[:], T.ysb[:]).then_inc(sem.sto, 16)
    sy.wait_ge(sem.sto, 16)
